import numpy as np
import ml_dtypes


def mxq(x, axis, fmt="e4m3"):
    dtype, down = {"e4m3": (ml_dtypes.float8_e4m3fn, 7), "e5m2": (ml_dtypes.float8_e5m2, 14)}[fmt]
    v = np.moveaxis(np.asarray(x, np.float32).astype(ml_dtypes.bfloat16).astype(np.float64), axis, -1)
    blocks = v.reshape(v.shape[:-1] + (-1, 32))
    amax = np.abs(blocks).max(-1, keepdims=True)
    byte = np.maximum(np.where(amax > 0, np.frexp(amax)[1] - 1 + 127, 0) - down, 1)
    scale = np.exp2(byte - 127.0)
    codes = (blocks / scale).astype(np.float32).astype(dtype).astype(np.float64)
    return np.moveaxis((codes * scale).reshape(v.shape), -1, axis)


WIDE = False


def mx_kscale(k):
    if not WIDE:
        return np.ones(k)
    levels = np.array([10, -10, 5, -5, 0])
    if k % 512:
        return np.exp2(np.random.permutation(np.resize(levels, k // 32))).repeat(32)
    a = np.empty((k // 512, 16))
    for p in range(k // 512):
        a[p, :8] = np.random.permutation(np.resize(levels, 8))
        for g in range(8):
            far = levels[np.abs(levels - a[p, g]) >= 10]
            a[p, g + 8] = far[np.random.randint(len(far))]
    return np.exp2(a.ravel()).repeat(32)


BF16 = ml_dtypes.bfloat16


def bf(x):
    return np.asarray(x, np.float32).astype(BF16)


def f64(x):
    return np.asarray(x).astype(np.float64)


E2M1 = np.array([0.0, 0.5, 1.0, 1.5, 2.0, 3.0, 4.0, 6.0, -0.0, -0.5, -1.0, -1.5, -2.0, -3.0, -4.0, -6.0])


def pack_weight(w, fmt):
    k, n = w.shape
    w = f64(bf(w)).reshape(k // 32, 32, n)
    amax = np.abs(w).max(1)
    if fmt == "e4m3":
        byte = np.frexp(amax)[1] - 1 + 127 - 7
    else:
        mant, ex = np.frexp(amax / 6.0)
        byte = np.where(mant > 0.5, ex, ex - 1) + 127
    byte = np.clip(np.where(amax > 0, byte, 1), 1, 254)
    scaled = (w * np.exp2(127.0 - byte)[:, None, :]).reshape(k, n).astype(np.float32)
    by_word = np.ascontiguousarray(scaled.reshape(k // 512, 128, 4, n).transpose(0, 1, 3, 2))
    if fmt == "e4m3":
        words = by_word.astype(ml_dtypes.float8_e4m3fn).view(np.uint8)
    else:
        c = by_word.astype(ml_dtypes.float4_e2m1fn).view(np.uint8) & 0xF
        words = c[..., 0::2] | (c[..., 1::2] << 4)
    return np.ascontiguousarray(words), np.ascontiguousarray(byte.astype(np.uint8).reshape(k // 512, 16, n))


def unpack_weight(words, scales, fmt):
    g, p, n, _ = words.shape
    if fmt == "e4m3":
        vals = np.ascontiguousarray(words).view(ml_dtypes.float8_e4m3fn).astype(np.float64)
    else:
        nib = np.empty((g, p, n, 4), np.uint8)
        nib[..., 0::2] = words & 0xF
        nib[..., 1::2] = words >> 4
        vals = E2M1[nib]
    vals = vals * np.repeat(np.exp2(scales.astype(np.float64) - 127.0), 8, axis=1)[..., None]
    return vals.transpose(0, 1, 3, 2).reshape(g * 512, n)

E4M3FN = np.array([(-1.0 if i & 128 else 1.0) * ((1.0 + (i & 7) / 8.0) * 2.0 ** (((i >> 3) & 15) - 7) if i & 120 else (i & 7) * 2.0 ** -9) for i in range(256)])


def e4m3fn_bytes(y):
    return np.clip(np.asarray(y, np.float64), -448.0, 448.0).astype(np.float32).astype(ml_dtypes.float8_e4m3fn).view(np.uint8)


def e4m3fn_values(b):
    return E4M3FN[b]


NE, NV, NF, C, F = 1536, 1024, 1024, 512, 512


def draw0():
    s0, s2 = mx_kscale(C), mx_kscale(C)
    t0, t2 = mx_kscale(NV), mx_kscale(NF)
    x0 = bf(np.random.standard_normal((NV, C)) * s0[None, :] * t0[:, None])
    x1 = bf(np.random.standard_normal((NE, F)))
    x2 = bf(np.random.standard_normal((NF, C)) * s2[None, :] * t2[:, None])
    inc_down = bf(np.random.standard_normal((NE, NV)) / np.sqrt(NV) / t0[None, :])
    inc_up = bf(np.random.standard_normal((NE, NF)) / np.sqrt(NF) / t2[None, :])
    w0_words, w0_scales = pack_weight(np.random.standard_normal((C, F)) / np.sqrt(C) / s0[:, None], "e4m3")
    w2_words, w2_scales = pack_weight(np.random.standard_normal((C, F)) / np.sqrt(C) / s2[:, None], "e4m3")
    return {
        "x0": x0,
        "x1": x1,
        "x2": x2,
        "inc_down": inc_down,
        "inc_up": inc_up,
        "w0_words": w0_words,
        "w0_scales": w0_scales,
        "w2_words": w2_words,
        "w2_scales": w2_scales,
    }


def incidence_message(incidence, cells, weight_words, weight_scales):
    h = mxq(f64(cells), 1, "e4m3") @ unpack_weight(weight_words, weight_scales, "e4m3")
    return mxq(f64(incidence), 1, "e4m3") @ mxq(h, 0, "e4m3")


def core(x0, x1, x2, inc_down, inc_up, w0_words, w0_scales, w2_words, w2_scales):
    m_down = incidence_message(inc_down, x0, w0_words, w0_scales)
    m_up = incidence_message(inc_up, x2, w2_words, w2_scales)
    z = f64(x1) + m_down + m_up
    return z * (1.0 / (1.0 + np.exp(-z)))


def setup_inputs():
    drawn = draw0()
    full = np.asarray(drawn['inc_up']).astype(np.float64)
    scale = (np.abs(full).reshape(1536, 8, 128).max(axis=(2,)) / 448.0).astype(np.float32)
    given = {}
    for key, value in drawn.items():
        if key == 'inc_up':
            given['inc_up_bytes'] = e4m3fn_bytes(full / np.repeat(scale.astype(np.float64), 128, axis=1))
            given['inc_up_scale'] = scale
        else:
            given[key] = value
    return given


def reference(x0, x1, x2, inc_down, inc_up_bytes, inc_up_scale, w0_words, w0_scales, w2_words, w2_scales):
    return core(x0, x1, x2, inc_down, e4m3fn_values(inc_up_bytes) * np.repeat(inc_up_scale.astype(np.float64), 128, axis=1), w0_words, w0_scales, w2_words, w2_scales)

@@ -1,0 +1,344 @@
+from contextlib import ExitStack
+
+import concourse.mybir as mybir
+from concourse.masks import make_identity
+
+F32 = mybir.dt.float32
+BF16 = mybir.dt.bfloat16
+U32 = mybir.dt.uint32
+I32 = mybir.dt.int32
+U8 = mybir.dt.uint8
+FP8 = mybir.dt.float8_e4m3fn
+FP8X4 = mybir.dt.float8_e4m3fn_x4
+ADD = mybir.AluOpType.add
+MULT = mybir.AluOpType.mult
+SILU = mybir.ActivationFunctionType.Silu
+
+P = 128
+NE, NV, C, F = 1536, 1024, 512, 512
+TILES = NE // P
+PAIRS = TILES // 2
+FLOPS = 2 * 2 * NV * C * F + 2 * 2 * NE * NV * F
+
+
+def tile_simplicialboundarycoboundarymessage_d1p_kernel(
+    tc, x0, x1, x2, inc_down, inc_up_bytes, inc_up_scale, w0_words, w0_scales, w2_words, w2_scales, out
+):
+    nc = tc.nc
+    with ExitStack() as ctx:
+        keep = ctx.enter_context(tc.tile_pool(name="keep", bufs=1))
+        work = ctx.enter_context(tc.tile_pool(name="work", bufs=3))
+        turned = ctx.enter_context(tc.psum_pool(name="turned", bufs=4))
+        sums = ctx.enter_context(tc.psum_pool(name="sums", bufs=4))
+        ctx.enter_context(tc.manual_schedule())
+
+        ident = keep.tile([P, P], F32, name="ident")
+        make_identity(nc, ident[:])
+        warm = keep.tile([P, 1], F32, name="warm")
+        nc.vector.memset(warm[:], 0.0)
+        nc.scalar.activation(out=warm[:], in_=warm[:], func=SILU)
+
+        w_scales = keep.tile([P, 2, F], U8, name="w_scales", align_bytes=64)
+        nc.vector.memset(w_scales[:].rearrange("p s n -> p (s n)").bitcast(I32), 0)
+        for s, src in enumerate((w0_scales, w2_scales)):
+            for q in range(4):
+                nc.scalar.dma_start(
+                    out=w_scales[32 * q : 32 * q + 4, s, :].bitcast(I32),
+                    in_=src[0, 4 * q : 4 * q + 4, :].bitcast(I32),
+                )
+        up_scale = keep.tile([P, TILES, 8], F32, name="up_scale")
+        nc.scalar.dma_start(out=up_scale[:], in_=inc_up_scale.rearrange("(m j) q -> m j q", j=TILES))
+
+        x_raw = [keep.tile([P, 4, C], BF16, name="x_raw%d" % c) for c in range(4)]
+        w_codes = [keep.tile([P, F], U32, name="w_codes%d" % s, align_bytes=64) for s in range(2)]
+        down_raw = [keep.tile([P, 2, NV], BF16, name="down_raw%d" % i) for i in range(PAIRS)]
+        up_raw = [keep.tile([P, 2, NV], U8, name="up_raw%d" % i) for i in range(PAIRS)]
+        edge = [keep.tile([P, 4, F], BF16, name="edge%d" % i) for i in range(3)]
+        down_rows = inc_down.rearrange("(m j) k -> m j k", j=TILES)
+        up_rows = inc_up_bytes.rearrange("(m j) k -> m j k", j=TILES)
+        x1_rows = x1.rearrange("(m j) f -> m j f", j=TILES)
+        out_rows = out.rearrange("(m j) f -> m j f", j=TILES)
+
+        def load_x(c, lo, hi):
+            rows = (x0, x2)[c // 2].rearrange("(g m t) c -> g m t c", m=P, t=4)[c % 2]
+            nc.sync.dma_start(out=x_raw[c][:, lo:hi, :], in_=rows[:, lo:hi, :])
+
+        def load_w(s):
+            words = (w0_words, w2_words)[s][0].rearrange("p n t -> p (n t)").bitcast(I32)
+            nc.sync.dma_start(out=w_codes[s][:].bitcast(I32), in_=words)
+
+        def load_down(i):
+            nc.sync.dma_start(out=down_raw[i][:], in_=down_rows[:, 2 * i : 2 * i + 2, :])
+
+        def load_up(i):
+            nc.sync.dma_start(out=up_raw[i][:], in_=up_rows[:, 2 * i : 2 * i + 2, :])
+
+        def load_edge(i):
+            nc.sync.dma_start(out=edge[i][:], in_=x1_rows[:, 4 * i : 4 * i + 4, :])
+
+        load_x(0, 0, 2)
+        load_x(0, 2, 4)
+        load_up(0)
+        load_x(1, 0, 2)
+        load_x(1, 2, 4)
+        load_w(0)
+        load_x(2, 0, 2)
+        load_x(2, 2, 4)
+        load_w(1)
+        load_down(0)
+        load_x(3, 0, 4)
+        load_up(1)
+        load_down(1)
+        load_edge(0)
+        load_up(2)
+        load_down(2)
+        load_up(3)
+        load_down(3)
+        load_edge(1)
+        load_up(4)
+        load_down(4)
+        load_up(5)
+        load_down(5)
+        load_edge(2)
+
+        def empty(engine, out_ap, in_ap):
+            if engine == "v":
+                nc.vector.tensor_copy(out=out_ap, in_=in_ap)
+            else:
+                nc.scalar.copy(out=out_ap, in_=in_ap)
+
+        x_turned = {}
+        x_grouped = {}
+        x_codes = {}
+        x_planes = {}
+
+        def turn_x(c):
+            words = x_raw[c][:].rearrange("m t c -> m (t c)").bitcast(F32)
+            banks = []
+            for half in range(2):
+                bank = turned.tile([P, 2, 256], F32, name="bank")
+                for t in range(2):
+                    base = 256 * (2 * half + t)
+                    for u in range(2):
+                        nc.tensor.transpose(bank[:, u, 128 * t : 128 * t + 128], words[:, base + u : base + 256 : 2], ident[:])
+                banks.append(bank)
+            x_turned[c] = banks
+
+        def empty_x(c, engines):
+            grouped = work.tile([P, 2048], BF16, name="x_grouped", align_bytes=64)
+            view = grouped[:].bitcast(F32).rearrange("p (h x u) -> p h x u", h=2, u=2)
+            for half in range(2):
+                empty(engines[half], view[:, half], x_turned[c][half][:].rearrange("p u x -> p x u"))
+            x_grouped[c] = grouped
+
+        def quantize_x(c):
+            x_codes[c] = work.tile([P, 512], U32, name="x_codes", align_bytes=64)
+            x_planes[c] = work.tile([P, 512], U8, name="x_planes", align_bytes=64)
+            nc.vector.quantize_mx(out=x_codes[c][:].bitcast(FP8X4), scales=x_planes[c][:], in_=x_grouped[c][:])
+
+        h_sums = {}
+        h_grouped = {}
+        h_codes = {}
+        h_planes = {}
+
+        def project(c):
+            banks = []
+            s = c // 2
+            for f in range(4):
+                cols = slice(128 * f, 128 * f + 128)
+                bank = sums.tile([P, 4, 128], F32, name="acc")
+                for t in range(4):
+                    rows = slice(128 * t, 128 * t + 128)
+                    nc.tensor.matmul_mx(
+                        out=bank[:, t, :],
+                        lhsT=x_codes[c][:, rows].bitcast(FP8X4),
+                        lhsT_scale=x_planes[c][:, rows],
+                        rhs=w_codes[s][:, cols].bitcast(FP8X4),
+                        rhs_scale=w_scales[:, s, cols],
+                        start=True,
+                        stop=True,
+                    )
+                banks.append(bank)
+            h_sums[c] = banks
+
+        def empty_h(c, engines):
+            grouped = work.tile([P, 512, 4], BF16, name="h_grouped", align_bytes=64)
+            for f in range(4):
+                empty(engines[f], grouped[:, 128 * f : 128 * f + 128, :], h_sums[c][f][:].rearrange("p t n -> p n t"))
+            h_grouped[c] = grouped
+
+        def quantize_h(c):
+            h_codes[c] = keep.tile([P, 512], U32, name="h_codes%d" % c, align_bytes=64)
+            h_planes[c] = keep.tile([P, 512], U8, name="h_planes%d" % c, align_bytes=64)
+            nc.vector.quantize_mx(
+                out=h_codes[c][:].bitcast(FP8X4), scales=h_planes[c][:], in_=h_grouped[c][:].rearrange("p n t -> p (n t)")
+            )
+
+        wide = {}
+
+        def widen(j):
+            tile = work.tile([P, 2, 2, 128, 2], BF16, name="wide", bufs=4)
+            raw = up_raw[j // 2]
+            for b in range(8):
+                g, q = divmod(b, 4)
+                nc.vector.tensor_scalar(
+                    out=tile[:, g, :, 32 * q : 32 * q + 32, :].rearrange("m u p e -> m p u e"),
+                    in0=raw[:, j % 2, 128 * b : 128 * b + 128].bitcast(FP8).rearrange("m (p u e) -> m p u e", u=2, e=2),
+                    scalar1=up_scale[:, j, b : b + 1],
+                    scalar2=None,
+                    op0=MULT,
+                )
+            wide[j] = tile
+
+        i_turned = {}
+        i_grouped = {}
+        i_codes = {}
+        i_planes = {}
+
+        def turn_down(i):
+            for k in range(2):
+                j = 2 * i + k
+                words = down_raw[i][:, k, :].bitcast(F32)
+                bank = turned.tile([P, 2, 256], F32, name="bank")
+                for g in range(2):
+                    for u in range(2):
+                        nc.tensor.transpose(
+                            bank[:, u, 128 * g : 128 * g + 128], words[:, 256 * g + u : 256 * g + 256 : 2], ident[:]
+                        )
+                i_turned[0, j] = bank
+
+        def turn_up(i):
+            for k in range(2):
+                j = 2 * i + k
+                words = wide[j][:].rearrange("m g u p e -> m (g u p e)").bitcast(F32)
+                bank = turned.tile([P, 2, 256], F32, name="bank")
+                for g in range(2):
+                    for u in range(2):
+                        lo = 256 * g + 128 * u
+                        nc.tensor.transpose(bank[:, u, 128 * g : 128 * g + 128], words[:, lo : lo + 128], ident[:])
+                i_turned[1, j] = bank
+
+        def empty_inc(s, i, engines):
+            grouped = work.tile([P, 2048], BF16, name="i_grouped%d" % s, align_bytes=64)
+            view = grouped[:].bitcast(F32).rearrange("p (h x u) -> p h x u", h=2, u=2)
+            for k in range(2):
+                empty(engines[k], view[:, k], i_turned[s, 2 * i + k][:].rearrange("p u x -> p x u"))
+            i_grouped[s, i] = grouped
+
+        def quantize_inc(s, i):
+            i_codes[s, i] = work.tile([P, 512], U32, name="i_codes%d" % s, align_bytes=64)
+            i_planes[s, i] = work.tile([P, 512], U8, name="i_planes%d" % s, align_bytes=64)
+            nc.vector.quantize_mx(
+                out=i_codes[s, i][:].bitcast(FP8X4), scales=i_planes[s, i][:], in_=i_grouped[s, i][:]
+            )
+
+        z_sums = {}
+
+        def carry(j):
+            i, k = divmod(j, 2)
+            bank = sums.tile([P, 512], F32, name="acc")
+            for c in range(4):
+                s, g = divmod(c, 2)
+                lo = 256 * k + 128 * g
+                nc.tensor.matmul_mx(
+                    out=bank[:],
+                    lhsT=i_codes[s, i][:, lo : lo + 128].bitcast(FP8X4),
+                    lhsT_scale=i_planes[s, i][:, lo : lo + 128],
+                    rhs=h_codes[c][:].bitcast(FP8X4),
+                    rhs_scale=h_planes[c][:],
+                    start=(c == 0),
+                    stop=(c == 3),
+                )
+            z_sums[j] = bank
+
+        z_tiles = {}
+
+        def add_edge(j):
+            z = work.tile([P, F], F32, name="z", bufs=5)
+            nc.vector.tensor_tensor(out=z[:], in0=z_sums[j][:], in1=edge[j // 4][:, j % 4, :], op=ADD)
+            z_tiles[j] = z
+
+        def finish(j):
+            result = keep.tile([P, F], F32, name="result%d" % j)
+            nc.scalar.activation(out=result[:], in_=z_tiles[j][:], func=SILU)
+            nc.sync.dma_start(out=out_rows[:, j, :], in_=result[:])
+
+        turn_x(0)
+        empty_x(0, "ss")
+        widen(0)
+        turn_x(1)
+        quantize_x(0)
+        empty_x(1, "ss")
+        widen(1)
+        project(0)
+        quantize_x(1)
+        empty_h(0, "svsv")
+        turn_x(2)
+        project(1)
+        empty_x(2, "sv")
+        quantize_h(0)
+        empty_h(1, "svsv")
+        quantize_x(2)
+        turn_x(3)
+        turn_down(0)
+        empty_x(3, "sv")
+        project(2)
+        quantize_h(1)
+        empty_inc(0, 0, "ss")
+        quantize_x(3)
+        empty_h(2, "svsv")
+        turn_up(0)
+        project(3)
+        widen(2)
+        empty_inc(1, 0, "ss")
+        quantize_inc(0, 0)
+        quantize_h(2)
+        widen(3)
+        empty_h(3, "svsv")
+        quantize_inc(1, 0)
+        turn_down(1)
+        turn_up(1)
+        quantize_h(3)
+        empty_inc(0, 1, "ss")
+        widen(4)
+        empty_inc(1, 1, "ss")
+        quantize_inc(0, 1)
+        widen(5)
+        for i in range(PAIRS):
+            ahead = i + 2 if 0 < i < PAIRS - 2 else None
+            if ahead:
+                turn_down(ahead)
+                turn_up(ahead)
+            if i > 0:
+                finish(2 * i - 2)
+                add_edge(2 * i - 1)
+            if ahead:
+                empty_inc(0, ahead, "ss")
+            if i > 0:
+                finish(2 * i - 1)
+            if ahead:
+                empty_inc(1, ahead, "ss")
+            if i == 0:
+                quantize_inc(1, 1)
+            carry(2 * i)
+            carry(2 * i + 1)
+            if i == 0:
+                turn_down(2)
+                turn_up(2)
+                empty_inc(0, 2, "ss")
+                empty_inc(1, 2, "ss")
+            if i + 3 < PAIRS:
+                widen(2 * i + 6)
+                widen(2 * i + 7)
+            if ahead:
+                quantize_inc(0, ahead)
+            if i == 0:
+                quantize_inc(0, 2)
+            add_edge(2 * i)
+            if ahead:
+                quantize_inc(1, ahead)
+            if i == 0:
+                quantize_inc(1, 2)
+        finish(TILES - 2)
+        add_edge(TILES - 1)
+        finish(TILES - 1)

@@ -40,14 +40,7 @@ def tile_simplicialboundarycoboundarymessage_d1p_kernel(
 
         w_scales = keep.tile([P, 2, F], U8, name="w_scales", align_bytes=64)
         nc.vector.memset(w_scales[:].rearrange("p s n -> p (s n)").bitcast(I32), 0)
-        for s, src in enumerate((w0_scales, w2_scales)):
-            for q in range(4):
-                nc.scalar.dma_start(
-                    out=w_scales[32 * q : 32 * q + 4, s, :].bitcast(I32),
-                    in_=src[0, 4 * q : 4 * q + 4, :].bitcast(I32),
-                )
         up_scale = keep.tile([P, TILES, 8], F32, name="up_scale")
-        nc.scalar.dma_start(out=up_scale[:], in_=inc_up_scale.rearrange("(m j) q -> m j q", j=TILES))
 
         x_raw = [keep.tile([P, 4, C], BF16, name="x_raw%d" % c) for c in range(4)]
         w_codes = [keep.tile([P, F], U32, name="w_codes%d" % s, align_bytes=64) for s in range(2)]
@@ -67,6 +60,16 @@ def tile_simplicialboundarycoboundarymessage_d1p_kernel(
             words = (w0_words, w2_words)[s][0].rearrange("p n t -> p (n t)").bitcast(I32)
             nc.sync.dma_start(out=w_codes[s][:].bitcast(I32), in_=words)
 
+        def load_planes(s):
+            for q in range(4):
+                nc.sync.dma_start(
+                    out=w_scales[32 * q : 32 * q + 4, s, :].bitcast(I32),
+                    in_=(w0_scales, w2_scales)[s][0, 4 * q : 4 * q + 4, :].bitcast(I32),
+                )
+
+        def load_scale():
+            nc.sync.dma_start(out=up_scale[:], in_=inc_up_scale.rearrange("(m j) q -> m j q", j=TILES))
+
         def load_down(i):
             nc.sync.dma_start(out=down_raw[i][:], in_=down_rows[:, 2 * i : 2 * i + 2, :])
 
@@ -78,15 +81,17 @@ def tile_simplicialboundarycoboundarymessage_d1p_kernel(
 
         load_x(0, 0, 2)
         load_x(0, 2, 4)
-        load_up(0)
         load_x(1, 0, 2)
         load_x(1, 2, 4)
+        load_planes(0)
         load_w(0)
-        load_x(2, 0, 2)
-        load_x(2, 2, 4)
+        load_x(2, 0, 4)
+        load_scale()
+        load_up(0)
         load_w(1)
-        load_down(0)
         load_x(3, 0, 4)
+        load_planes(1)
+        load_down(0)
         load_up(1)
         load_down(1)
         load_edge(0)
@@ -264,21 +269,21 @@ def tile_simplicialboundarycoboundarymessage_d1p_kernel(
             nc.sync.dma_start(out=out_rows[:, j, :], in_=result[:])
 
         turn_x(0)
-        empty_x(0, "ss")
-        widen(0)
+        empty_x(0, "sv")
         turn_x(1)
         quantize_x(0)
-        empty_x(1, "ss")
-        widen(1)
+        empty_x(1, "sv")
         project(0)
         quantize_x(1)
-        empty_h(0, "svsv")
+        empty_h(0, "svss")
+        widen(0)
         turn_x(2)
         project(1)
         empty_x(2, "sv")
         quantize_h(0)
         empty_h(1, "svsv")
         quantize_x(2)
+        widen(1)
         turn_x(3)
         turn_down(0)
         empty_x(3, "sv")

@@ -34,6 +34,8 @@ def tile_simplicialboundarycoboundarymessage_d1p_kernel(
 
         ident = keep.tile([P, P], F32, name="ident")
         make_identity(nc, ident[:])
+        idle = keep.tile([P, F], BF16, name="idle")
+        nc.vector.memset(idle[:], 0.0)
         warm = keep.tile([P, 1], F32, name="warm")
         nc.vector.memset(warm[:], 0.0)
         nc.scalar.activation(out=warm[:], in_=warm[:], func=SILU)
@@ -111,6 +113,11 @@ def tile_simplicialboundarycoboundarymessage_d1p_kernel(
                 nc.vector.tensor_copy(out=out_ap, in_=in_ap)
             else:
                 nc.scalar.copy(out=out_ap, in_=in_ap)
+
+        def warm_up(n):
+            bank = sums.tile([P, F], F32, name="acc")
+            for k in range(n):
+                nc.tensor.matmul(bank[:], lhsT=idle[:, :P], rhs=idle[:], start=True, stop=True)
 
         x_turned = {}
         x_grouped = {}
@@ -239,38 +246,42 @@ def tile_simplicialboundarycoboundarymessage_d1p_kernel(
 
         z_sums = {}
 
-        def carry(j):
+        def carry(j, lo=0, width=F):
             i, k = divmod(j, 2)
-            bank = sums.tile([P, 512], F32, name="acc")
+            cols = slice(lo, lo + width)
+            bank = sums.tile([P, width], F32, name="acc")
             for c in range(4):
                 s, g = divmod(c, 2)
-                lo = 256 * k + 128 * g
+                first = 256 * k + 128 * g
                 nc.tensor.matmul_mx(
                     out=bank[:],
-                    lhsT=i_codes[s, i][:, lo : lo + 128].bitcast(FP8X4),
-                    lhsT_scale=i_planes[s, i][:, lo : lo + 128],
-                    rhs=h_codes[c][:].bitcast(FP8X4),
-                    rhs_scale=h_planes[c][:],
+                    lhsT=i_codes[s, i][:, first : first + 128].bitcast(FP8X4),
+                    lhsT_scale=i_planes[s, i][:, first : first + 128],
+                    rhs=h_codes[c][:, cols].bitcast(FP8X4),
+                    rhs_scale=h_planes[c][:, cols],
                     start=(c == 0),
                     stop=(c == 3),
                 )
-            z_sums[j] = bank
+            z_sums[j, lo] = bank
 
         z_tiles = {}
 
-        def add_edge(j):
-            z = work.tile([P, F], F32, name="z", bufs=5)
-            nc.vector.tensor_tensor(out=z[:], in0=z_sums[j][:], in1=edge[j // 4][:, j % 4, :], op=ADD)
-            z_tiles[j] = z
+        def add_edge(j, lo=0, width=F):
+            z = work.tile([P, width], F32, name="z", bufs=5)
+            nc.vector.tensor_tensor(out=z[:], in0=z_sums[j, lo][:], in1=edge[j // 4][:, j % 4, lo : lo + width], op=ADD)
+            z_tiles[j, lo] = z
 
-        def finish(j):
-            result = keep.tile([P, F], F32, name="result%d" % j)
-            nc.scalar.activation(out=result[:], in_=z_tiles[j][:], func=SILU)
-            nc.sync.dma_start(out=out_rows[:, j, :], in_=result[:])
+        def finish(j, lo=0, width=F):
+            result = keep.tile([P, width], F32, name="result%d_%d" % (j, lo))
+            nc.scalar.activation(out=result[:], in_=z_tiles[j, lo][:], func=SILU)
+            nc.sync.dma_start(out=out_rows[:, j, lo : lo + width], in_=result[:])
 
+        warm_up(4)
         turn_x(0)
+        warm_up(2)
         empty_x(0, "sv")
         turn_x(1)
+        warm_up(2)
         quantize_x(0)
         empty_x(1, "sv")
         project(0)
@@ -279,19 +290,19 @@ def tile_simplicialboundarycoboundarymessage_d1p_kernel(
         widen(0)
         turn_x(2)
         project(1)
-        empty_x(2, "sv")
+        empty_x(2, "ss")
         quantize_h(0)
-        empty_h(1, "svsv")
+        empty_h(1, "svss")
         quantize_x(2)
         widen(1)
         turn_x(3)
-        turn_down(0)
-        empty_x(3, "sv")
+        empty_x(3, "ss")
         project(2)
         quantize_h(1)
-        empty_inc(0, 0, "ss")
         quantize_x(3)
-        empty_h(2, "svsv")
+        empty_h(2, "svss")
+        turn_down(0)
+        empty_inc(0, 0, "ss")
         turn_up(0)
         project(3)
         widen(2)
@@ -299,7 +310,7 @@ def tile_simplicialboundarycoboundarymessage_d1p_kernel(
         quantize_inc(0, 0)
         quantize_h(2)
         widen(3)
-        empty_h(3, "svsv")
+        empty_h(3, "svss")
         quantize_inc(1, 0)
         turn_down(1)
         turn_up(1)
@@ -326,7 +337,11 @@ def tile_simplicialboundarycoboundarymessage_d1p_kernel(
             if i == 0:
                 quantize_inc(1, 1)
             carry(2 * i)
-            carry(2 * i + 1)
+            if i + 1 < PAIRS:
+                carry(2 * i + 1)
+            else:
+                for lo in (0, 256):
+                    carry(TILES - 1, lo, 256)
             if i == 0:
                 turn_down(2)
                 turn_up(2)
@@ -345,5 +360,6 @@ def tile_simplicialboundarycoboundarymessage_d1p_kernel(
             if i == 0:
                 quantize_inc(1, 2)
         finish(TILES - 2)
-        add_edge(TILES - 1)
-        finish(TILES - 1)
+        for lo in (0, 256):
+            add_edge(TILES - 1, lo, 256)
+            finish(TILES - 1, lo, 256)

@@ -81,7 +81,8 @@ def tile_simplicialboundarycoboundarymessage_d1p_kernel(
         def load_edge(i):
             nc.sync.dma_start(out=edge[i][:], in_=x1_rows[:, 4 * i : 4 * i + 4, :])
 
-        load_x(0, 0, 2)
+        load_x(0, 0, 1)
+        load_x(0, 1, 2)
         load_x(0, 2, 4)
         load_x(1, 0, 2)
         load_x(1, 2, 4)
@@ -278,48 +279,47 @@ def tile_simplicialboundarycoboundarymessage_d1p_kernel(
 
         warm_up(4)
         turn_x(0)
+        empty_x(0, "vv")
         warm_up(2)
-        empty_x(0, "sv")
         turn_x(1)
-        warm_up(2)
         quantize_x(0)
         empty_x(1, "sv")
         project(0)
-        quantize_x(1)
         empty_h(0, "svss")
-        widen(0)
         turn_x(2)
-        project(1)
+        quantize_x(1)
         empty_x(2, "ss")
-        quantize_h(0)
-        empty_h(1, "svss")
-        quantize_x(2)
         widen(1)
+        project(1)
+        widen(0)
+        quantize_x(2)
+        empty_h(1, "sssv")
         turn_x(3)
-        empty_x(3, "ss")
+        empty_x(3, "vs")
         project(2)
         quantize_h(1)
-        quantize_x(3)
-        empty_h(2, "svss")
         turn_down(0)
+        quantize_h(0)
+        empty_h(2, "svss")
         empty_inc(0, 0, "ss")
         turn_up(0)
-        project(3)
-        widen(2)
+        quantize_x(3)
         empty_inc(1, 0, "ss")
-        quantize_inc(0, 0)
+        widen(2)
+        project(3)
         quantize_h(2)
+        turn_down(1)
+        quantize_inc(0, 0)
         widen(3)
         empty_h(3, "svss")
         quantize_inc(1, 0)
-        turn_down(1)
-        turn_up(1)
         quantize_h(3)
         empty_inc(0, 1, "ss")
-        widen(4)
-        empty_inc(1, 1, "ss")
-        quantize_inc(0, 1)
+        turn_up(1)
         widen(5)
+        quantize_inc(0, 1)
+        empty_inc(1, 1, "ss")
+        widen(4)
         for i in range(PAIRS):
             ahead = i + 2 if 0 < i < PAIRS - 2 else None
             if ahead:

from contextlib import ExitStack

import concourse.mybir as mybir
from concourse.masks import make_identity

F32 = mybir.dt.float32
BF16 = mybir.dt.bfloat16
U32 = mybir.dt.uint32
I32 = mybir.dt.int32
U8 = mybir.dt.uint8
FP8 = mybir.dt.float8_e4m3fn
FP8X4 = mybir.dt.float8_e4m3fn_x4
ADD = mybir.AluOpType.add
MULT = mybir.AluOpType.mult
SILU = mybir.ActivationFunctionType.Silu

P = 128
NE, NV, C, F = 1536, 1024, 512, 512
TILES = NE // P
PAIRS = TILES // 2
FLOPS = 2 * 2 * NV * C * F + 2 * 2 * NE * NV * F


def tile_simplicialboundarycoboundarymessage_d1p_kernel(
    tc, x0, x1, x2, inc_down, inc_up_bytes, inc_up_scale, w0_words, w0_scales, w2_words, w2_scales, out
):
    nc = tc.nc
    with ExitStack() as ctx:
        keep = ctx.enter_context(tc.tile_pool(name="keep", bufs=1))
        work = ctx.enter_context(tc.tile_pool(name="work", bufs=3))
        turned = ctx.enter_context(tc.psum_pool(name="turned", bufs=4))
        sums = ctx.enter_context(tc.psum_pool(name="sums", bufs=4))
        ctx.enter_context(tc.manual_schedule())

        ident = keep.tile([P, P], F32, name="ident")
        make_identity(nc, ident[:])
        idle = keep.tile([P, F], BF16, name="idle")
        nc.vector.memset(idle[:], 0.0)
        warm = keep.tile([P, 1], F32, name="warm")
        nc.vector.memset(warm[:], 0.0)
        nc.scalar.activation(out=warm[:], in_=warm[:], func=SILU)

        w_scales = keep.tile([P, 2, F], U8, name="w_scales", align_bytes=64)
        nc.vector.memset(w_scales[:].rearrange("p s n -> p (s n)").bitcast(I32), 0)
        up_scale = keep.tile([P, TILES, 8], F32, name="up_scale")

        x_raw = [keep.tile([P, 4, C], BF16, name="x_raw%d" % c) for c in range(4)]
        w_codes = [keep.tile([P, F], U32, name="w_codes%d" % s, align_bytes=64) for s in range(2)]
        down_raw = [keep.tile([P, 2, NV], BF16, name="down_raw%d" % i) for i in range(PAIRS)]
        up_raw = [keep.tile([P, 2, NV], U8, name="up_raw%d" % i) for i in range(PAIRS)]
        edge = [keep.tile([P, 4, F], BF16, name="edge%d" % i) for i in range(3)]
        down_rows = inc_down.rearrange("(m j) k -> m j k", j=TILES)
        up_rows = inc_up_bytes.rearrange("(m j) k -> m j k", j=TILES)
        x1_rows = x1.rearrange("(m j) f -> m j f", j=TILES)
        out_rows = out.rearrange("(m j) f -> m j f", j=TILES)

        def load_x(c, lo, hi):
            rows = (x0, x2)[c // 2].rearrange("(g m t) c -> g m t c", m=P, t=4)[c % 2]
            nc.sync.dma_start(out=x_raw[c][:, lo:hi, :], in_=rows[:, lo:hi, :])

        def load_w(s):
            words = (w0_words, w2_words)[s][0].rearrange("p n t -> p (n t)").bitcast(I32)
            nc.sync.dma_start(out=w_codes[s][:].bitcast(I32), in_=words)

        def load_planes(s):
            for q in range(4):
                nc.sync.dma_start(
                    out=w_scales[32 * q : 32 * q + 4, s, :].bitcast(I32),
                    in_=(w0_scales, w2_scales)[s][0, 4 * q : 4 * q + 4, :].bitcast(I32),
                )

        def load_scale():
            nc.sync.dma_start(out=up_scale[:], in_=inc_up_scale.rearrange("(m j) q -> m j q", j=TILES))

        def load_down(i):
            nc.sync.dma_start(out=down_raw[i][:], in_=down_rows[:, 2 * i : 2 * i + 2, :])

        def load_up(i):
            nc.sync.dma_start(out=up_raw[i][:], in_=up_rows[:, 2 * i : 2 * i + 2, :])

        def load_edge(i):
            nc.sync.dma_start(out=edge[i][:], in_=x1_rows[:, 4 * i : 4 * i + 4, :])

        load_x(0, 0, 1)
        load_x(0, 1, 2)
        load_x(0, 2, 4)
        load_x(1, 0, 2)
        load_x(1, 2, 4)
        load_planes(0)
        load_w(0)
        load_x(2, 0, 4)
        load_scale()
        load_up(0)
        load_w(1)
        load_x(3, 0, 4)
        load_planes(1)
        load_down(0)
        load_up(1)
        load_down(1)
        load_edge(0)
        load_up(2)
        load_down(2)
        load_up(3)
        load_down(3)
        load_edge(1)
        load_up(4)
        load_down(4)
        load_up(5)
        load_down(5)
        load_edge(2)

        def empty(engine, out_ap, in_ap):
            if engine == "v":
                nc.vector.tensor_copy(out=out_ap, in_=in_ap)
            else:
                nc.scalar.copy(out=out_ap, in_=in_ap)

        def warm_up(n):
            bank = sums.tile([P, F], F32, name="acc")
            for k in range(n):
                nc.tensor.matmul(bank[:], lhsT=idle[:, :P], rhs=idle[:], start=True, stop=True)

        x_turned = {}
        x_grouped = {}
        x_codes = {}
        x_planes = {}

        def turn_x(c):
            words = x_raw[c][:].rearrange("m t c -> m (t c)").bitcast(F32)
            banks = []
            for half in range(2):
                bank = turned.tile([P, 2, 256], F32, name="bank")
                for t in range(2):
                    base = 256 * (2 * half + t)
                    for u in range(2):
                        nc.tensor.transpose(bank[:, u, 128 * t : 128 * t + 128], words[:, base + u : base + 256 : 2], ident[:])
                banks.append(bank)
            x_turned[c] = banks

        def empty_x(c, engines):
            grouped = work.tile([P, 2048], BF16, name="x_grouped", align_bytes=64)
            view = grouped[:].bitcast(F32).rearrange("p (h x u) -> p h x u", h=2, u=2)
            for half in range(2):
                empty(engines[half], view[:, half], x_turned[c][half][:].rearrange("p u x -> p x u"))
            x_grouped[c] = grouped

        def quantize_x(c):
            x_codes[c] = work.tile([P, 512], U32, name="x_codes", align_bytes=64)
            x_planes[c] = work.tile([P, 512], U8, name="x_planes", align_bytes=64)
            nc.vector.quantize_mx(out=x_codes[c][:].bitcast(FP8X4), scales=x_planes[c][:], in_=x_grouped[c][:])

        h_sums = {}
        h_grouped = {}
        h_codes = {}
        h_planes = {}

        def project(c):
            banks = []
            s = c // 2
            for f in range(4):
                cols = slice(128 * f, 128 * f + 128)
                bank = sums.tile([P, 4, 128], F32, name="acc")
                for t in range(4):
                    rows = slice(128 * t, 128 * t + 128)
                    nc.tensor.matmul_mx(
                        out=bank[:, t, :],
                        lhsT=x_codes[c][:, rows].bitcast(FP8X4),
                        lhsT_scale=x_planes[c][:, rows],
                        rhs=w_codes[s][:, cols].bitcast(FP8X4),
                        rhs_scale=w_scales[:, s, cols],
                        start=True,
                        stop=True,
                    )
                banks.append(bank)
            h_sums[c] = banks

        def empty_h(c, engines):
            grouped = work.tile([P, 512, 4], BF16, name="h_grouped", align_bytes=64)
            for f in range(4):
                empty(engines[f], grouped[:, 128 * f : 128 * f + 128, :], h_sums[c][f][:].rearrange("p t n -> p n t"))
            h_grouped[c] = grouped

        def quantize_h(c):
            h_codes[c] = keep.tile([P, 512], U32, name="h_codes%d" % c, align_bytes=64)
            h_planes[c] = keep.tile([P, 512], U8, name="h_planes%d" % c, align_bytes=64)
            nc.vector.quantize_mx(
                out=h_codes[c][:].bitcast(FP8X4), scales=h_planes[c][:], in_=h_grouped[c][:].rearrange("p n t -> p (n t)")
            )

        wide = {}

        def widen(j):
            tile = work.tile([P, 2, 2, 128, 2], BF16, name="wide", bufs=4)
            raw = up_raw[j // 2]
            for b in range(8):
                g, q = divmod(b, 4)
                nc.vector.tensor_scalar(
                    out=tile[:, g, :, 32 * q : 32 * q + 32, :].rearrange("m u p e -> m p u e"),
                    in0=raw[:, j % 2, 128 * b : 128 * b + 128].bitcast(FP8).rearrange("m (p u e) -> m p u e", u=2, e=2),
                    scalar1=up_scale[:, j, b : b + 1],
                    scalar2=None,
                    op0=MULT,
                )
            wide[j] = tile

        i_turned = {}
        i_grouped = {}
        i_codes = {}
        i_planes = {}

        def turn_down(i):
            for k in range(2):
                j = 2 * i + k
                words = down_raw[i][:, k, :].bitcast(F32)
                bank = turned.tile([P, 2, 256], F32, name="bank")
                for g in range(2):
                    for u in range(2):
                        nc.tensor.transpose(
                            bank[:, u, 128 * g : 128 * g + 128], words[:, 256 * g + u : 256 * g + 256 : 2], ident[:]
                        )
                i_turned[0, j] = bank

        def turn_up(i):
            for k in range(2):
                j = 2 * i + k
                words = wide[j][:].rearrange("m g u p e -> m (g u p e)").bitcast(F32)
                bank = turned.tile([P, 2, 256], F32, name="bank")
                for g in range(2):
                    for u in range(2):
                        lo = 256 * g + 128 * u
                        nc.tensor.transpose(bank[:, u, 128 * g : 128 * g + 128], words[:, lo : lo + 128], ident[:])
                i_turned[1, j] = bank

        def empty_inc(s, i, engines):
            grouped = work.tile([P, 2048], BF16, name="i_grouped%d" % s, align_bytes=64)
            view = grouped[:].bitcast(F32).rearrange("p (h x u) -> p h x u", h=2, u=2)
            for k in range(2):
                empty(engines[k], view[:, k], i_turned[s, 2 * i + k][:].rearrange("p u x -> p x u"))
            i_grouped[s, i] = grouped

        def quantize_inc(s, i):
            i_codes[s, i] = work.tile([P, 512], U32, name="i_codes%d" % s, align_bytes=64)
            i_planes[s, i] = work.tile([P, 512], U8, name="i_planes%d" % s, align_bytes=64)
            nc.vector.quantize_mx(
                out=i_codes[s, i][:].bitcast(FP8X4), scales=i_planes[s, i][:], in_=i_grouped[s, i][:]
            )

        z_sums = {}

        def carry(j, lo=0, width=F):
            i, k = divmod(j, 2)
            cols = slice(lo, lo + width)
            bank = sums.tile([P, width], F32, name="acc")
            for c in range(4):
                s, g = divmod(c, 2)
                first = 256 * k + 128 * g
                nc.tensor.matmul_mx(
                    out=bank[:],
                    lhsT=i_codes[s, i][:, first : first + 128].bitcast(FP8X4),
                    lhsT_scale=i_planes[s, i][:, first : first + 128],
                    rhs=h_codes[c][:, cols].bitcast(FP8X4),
                    rhs_scale=h_planes[c][:, cols],
                    start=(c == 0),
                    stop=(c == 3),
                )
            z_sums[j, lo] = bank

        z_tiles = {}

        def add_edge(j, lo=0, width=F):
            z = work.tile([P, width], F32, name="z", bufs=5)
            nc.vector.tensor_tensor(out=z[:], in0=z_sums[j, lo][:], in1=edge[j // 4][:, j % 4, lo : lo + width], op=ADD)
            z_tiles[j, lo] = z

        def finish(j, lo=0, width=F):
            result = keep.tile([P, width], F32, name="result%d_%d" % (j, lo))
            nc.scalar.activation(out=result[:], in_=z_tiles[j, lo][:], func=SILU)
            nc.sync.dma_start(out=out_rows[:, j, lo : lo + width], in_=result[:])

        warm_up(4)
        turn_x(0)
        empty_x(0, "vv")
        warm_up(2)
        turn_x(1)
        quantize_x(0)
        empty_x(1, "sv")
        project(0)
        empty_h(0, "svss")
        turn_x(2)
        quantize_x(1)
        empty_x(2, "ss")
        widen(1)
        project(1)
        widen(0)
        quantize_x(2)
        empty_h(1, "sssv")
        turn_x(3)
        empty_x(3, "vs")
        project(2)
        quantize_h(1)
        turn_down(0)
        quantize_h(0)
        empty_h(2, "svss")
        empty_inc(0, 0, "ss")
        turn_up(0)
        quantize_x(3)
        empty_inc(1, 0, "ss")
        widen(2)
        project(3)
        quantize_h(2)
        turn_down(1)
        quantize_inc(0, 0)
        widen(3)
        empty_h(3, "svss")
        quantize_inc(1, 0)
        quantize_h(3)
        empty_inc(0, 1, "ss")
        turn_up(1)
        widen(5)
        quantize_inc(0, 1)
        empty_inc(1, 1, "ss")
        widen(4)
        for i in range(PAIRS):
            ahead = i + 2 if 0 < i < PAIRS - 2 else None
            if ahead:
                turn_down(ahead)
                turn_up(ahead)
            if i > 0:
                finish(2 * i - 2)
                add_edge(2 * i - 1)
            if ahead:
                empty_inc(0, ahead, "ss")
            if i > 0:
                finish(2 * i - 1)
            if ahead:
                empty_inc(1, ahead, "ss")
            if i == 0:
                quantize_inc(1, 1)
            carry(2 * i)
            if i + 1 < PAIRS:
                carry(2 * i + 1)
            else:
                for lo in (0, 256):
                    carry(TILES - 1, lo, 256)
            if i == 0:
                turn_down(2)
                turn_up(2)
                empty_inc(0, 2, "ss")
                empty_inc(1, 2, "ss")
            if i + 3 < PAIRS:
                widen(2 * i + 6)
                widen(2 * i + 7)
            if ahead:
                quantize_inc(0, ahead)
            if i == 0:
                quantize_inc(0, 2)
            add_edge(2 * i)
            if ahead:
                quantize_inc(1, ahead)
            if i == 0:
                quantize_inc(1, 2)
        finish(TILES - 2)
        for lo in (0, 256):
            add_edge(TILES - 1, lo, 256)
            finish(TILES - 1, lo, 256)
